import numpy as np
import ml_dtypes


def mxq(x, axis, fmt="e4m3"):
    dtype, down = {"e4m3": (ml_dtypes.float8_e4m3fn, 7), "e5m2": (ml_dtypes.float8_e5m2, 14)}[fmt]
    v = np.moveaxis(np.asarray(x, np.float32).astype(ml_dtypes.bfloat16).astype(np.float64), axis, -1)
    blocks = v.reshape(v.shape[:-1] + (-1, 32))
    amax = np.abs(blocks).max(-1, keepdims=True)
    byte = np.maximum(np.where(amax > 0, np.frexp(amax)[1] - 1 + 127, 0) - down, 1)
    scale = np.exp2(byte - 127.0)
    codes = (blocks / scale).astype(np.float32).astype(dtype).astype(np.float64)
    return np.moveaxis((codes * scale).reshape(v.shape), -1, axis)


WIDE = False


def mx_kscale(k):
    if not WIDE:
        return np.ones(k)
    levels = np.array([10, -10, 5, -5, 0])
    if k % 512:
        return np.exp2(np.random.permutation(np.resize(levels, k // 32))).repeat(32)
    a = np.empty((k // 512, 16))
    for p in range(k // 512):
        a[p, :8] = np.random.permutation(np.resize(levels, 8))
        for g in range(8):
            far = levels[np.abs(levels - a[p, g]) >= 10]
            a[p, g + 8] = far[np.random.randint(len(far))]
    return np.exp2(a.ravel()).repeat(32)


def f64(x):
    return np.asarray(x).astype(np.float64)


def striped(idx):
    return np.tile(idx.reshape(-1, 16).T, (8, 1)).astype(np.uint16)


def unstriped(offs):
    return offs[:16].T.reshape(-1).astype(np.int64)


E2M1 = np.array([0.0, 0.5, 1.0, 1.5, 2.0, 3.0, 4.0, 6.0, -0.0, -0.5, -1.0, -1.5, -2.0, -3.0, -4.0, -6.0])


def pack_weight(w, fmt):
    k, n = w.shape
    w = f64(np.asarray(w, np.float32).astype(ml_dtypes.bfloat16)).reshape(k // 32, 32, n)
    amax = np.abs(w).max(1)
    if fmt == "e4m3":
        byte = np.frexp(amax)[1] - 1 + 127 - 7
    else:
        mant, ex = np.frexp(amax / 6.0)
        byte = np.where(mant > 0.5, ex, ex - 1) + 127
    byte = np.clip(np.where(amax > 0, byte, 1), 1, 254)
    scaled = (w * np.exp2(127.0 - byte)[:, None, :]).reshape(k, n).astype(np.float32)
    by_word = np.ascontiguousarray(scaled.reshape(k // 512, 128, 4, n).transpose(0, 1, 3, 2))
    if fmt == "e4m3":
        words = by_word.astype(ml_dtypes.float8_e4m3fn).view(np.uint8)
    else:
        c = by_word.astype(ml_dtypes.float4_e2m1fn).view(np.uint8) & 0xF
        words = (c[..., 0::2] | (c[..., 1::2] << 4)).reshape(k // 512, 128, 2 * n)
    return np.ascontiguousarray(words), np.ascontiguousarray(byte.astype(np.uint8).reshape(k // 512, 16, n))


def unpack_weight(words, scales, fmt):
    g, _, n = scales.shape
    words = np.ascontiguousarray(words).reshape(g, 128, n, -1)
    if fmt == "e4m3":
        vals = words.view(ml_dtypes.float8_e4m3fn).astype(np.float64)
    else:
        nib = np.empty((g, 128, n, 4), np.uint8)
        nib[..., 0::2] = words & 0xF
        nib[..., 1::2] = words >> 4
        vals = E2M1[nib]
    vals = vals * np.repeat(np.exp2(scales.astype(np.float64) - 127.0), 8, axis=1)[..., None]
    return vals.transpose(0, 1, 3, 2).reshape(g * 512, n)


def gelu(v):
    return 0.5 * v * (1.0 + np.tanh(np.sqrt(2.0 / np.pi) * (v + 0.044715 * v**3)))


def twice(P):
    return np.random.permutation(np.repeat(np.arange(P), 2))


K, H, T, S, P = 1536, 1024, 4096, 1024, 512

def setup_inputs():
    n = np.random.standard_normal
    s = mx_kscale(K)[:, None]
    u = mx_kscale(H)[:, None]
    d = {}
    d["tab_words"], d["tab_scales"] = pack_weight(n((K, T)) * s, "e4m3")
    d["offs"] = striped(np.random.permutation(T)[:S])
    d["pos1"] = striped(np.random.permutation(S)[:P])
    d["pos2"] = striped(np.random.permutation(S)[:P])
    d["pos3"] = striped(twice(P))
    d["w1"] = (n((K, H)) / K**0.5 / s * u.T).astype(np.float32)
    d["wsum_words"], d["wsum_scales"] = pack_weight(n((H, H)) / H**0.5 / u, "e2m1")
    d["wdiff"] = (n((H, H)) / H**0.5 / u).astype(np.float32)
    d["gain"] = (0.6 * np.exp(0.5 * n(H)) / u[:, 0]).astype(np.float32)
    return d

def reference(tab_words, tab_scales, offs, pos1, pos2, pos3, w1, wsum_words, wsum_scales, wdiff, gain):
    v = unpack_weight(tab_words, tab_scales, "e4m3")[:, unstriped(offs)]
    h = mxq(f64(w1), 0, "e4m3").T @ v
    core = h[:, unstriped(pos1)]
    surf = h[:, unstriped(pos2)]
    both = mxq(core + surf, 0, "e4m3")
    drop = mxq(core - surf, 0, "e4m3")
    level = unpack_weight(wsum_words, wsum_scales, "e2m1").T @ both
    grad = mxq(f64(wdiff), 0, "e4m3").T @ drop
    y = np.maximum(level, grad)
    up = y[:, unstriped(pos3)]
    return np.log1p(np.square(up)) + f64(gain)[:, None] * h

@@ -1,0 +1,251 @@
+from contextlib import ExitStack
+
+import concourse.mybir as mybir
+
+K, H, T, S, SECT = 1536, 1024, 4096, 1024, 512
+FLOPS = 2 * K * H * S + 2 * 2 * H * H * SECT
+
+F32 = mybir.dt.float32
+BF16 = mybir.dt.bfloat16
+I32 = mybir.dt.int32
+U32 = mybir.dt.uint32
+U16 = mybir.dt.uint16
+U8 = mybir.dt.uint8
+FP8X4 = mybir.dt.float8_e4m3fn_x4
+FP4X4 = mybir.dt.float4_e2m1fn_x4
+ALU = mybir.AluOpType
+ACT = mybir.ActivationFunctionType
+
+P = 128
+PACK = 4
+KP = P * PACK
+BANK = 512
+PASSES1 = K // KP
+PASSES2 = H // KP
+VECTOR_SHARE = 84
+
+
+def tile_list_curing_crack_score_kernel(
+    tc, tab_words, tab_scales, offs, pos1, pos2, pos3, w1, wsum_words, wsum_scales, wdiff, gain, out
+):
+    nc = tc.nc
+    with ExitStack() as ctx:
+        keep = ctx.enter_context(tc.tile_pool(name="keep", bufs=1))
+        big = ctx.enter_context(tc.tile_pool(name="big", bufs=3))
+        rawp = ctx.enter_context(tc.tile_pool(name="rawp", bufs=8))
+        grp = ctx.enter_context(tc.tile_pool(name="grp", bufs=3))
+        psum = ctx.enter_context(tc.psum_pool(name="psum", bufs=8))
+
+        offs_t = keep.tile([P, S // 16], U16, name="offs_t")
+        pos1_t = keep.tile([P, SECT // 16], U16, name="pos1_t")
+        pos2_t = keep.tile([P, SECT // 16], U16, name="pos2_t")
+        pos3_t = keep.tile([P, S // 16], U16, name="pos3_t")
+        gain_t = keep.tile([P, PASSES2, PACK], F32, name="gain_t")
+        tab_sc = keep.tile([P, T], U8, name="tab_sc")
+        wsum_raw = keep.tile([P, PASSES2, 2 * H], U8, name="wsum_raw")
+        wsum_sc_raw = keep.tile([P, PASSES2, H], U8, name="wsum_sc_raw")
+
+        nc.vector.memset(tab_sc[:].bitcast(I32), 0)
+        nc.vector.memset(wsum_sc_raw[:].bitcast(I32), 0)
+
+        def load_table(a):
+            words = big.tile([P, T], U32, name="big")
+            nc.sync.dma_start(words[:].bitcast(I32), tab_words[a].rearrange("p t i -> p (t i)").bitcast(I32))
+            return words
+
+        def load_weight(w, a, b):
+            raw = rawp.tile([P, PACK, KP], F32, name="raw")
+            nc.sync.dma_start(
+                raw[:], w[a * KP : (a + 1) * KP, b * KP : (b + 1) * KP].rearrange("(p j) c -> p j c", j=PACK)
+            )
+            return raw
+
+        tab = [None] * PASSES1
+        w1_raw = {}
+        wd_raw = {}
+        nc.sync.dma_start(offs_t[:], offs)
+        tab[0] = load_table(0)
+        for q in range(4):
+            nc.sync.dma_start(
+                tab_sc[32 * q : 32 * q + 4 * PASSES1, :].bitcast(I32),
+                tab_scales[:, 4 * q : 4 * q + 4, :].bitcast(I32),
+            )
+        w1_raw[0, 0] = load_weight(w1, 0, 0)
+        tab[1] = load_table(1)
+        w1_raw[1, 0] = load_weight(w1, 1, 0)
+        for q in range(4):
+            nc.sync.dma_start(
+                wsum_sc_raw[32 * q : 32 * q + 4, :, :].bitcast(I32),
+                wsum_scales[:, 4 * q : 4 * q + 4, :].rearrange("a r c -> r a c").bitcast(I32),
+            )
+        tab[2] = load_table(2)
+        w1_raw[2, 0] = load_weight(w1, 2, 0)
+        nc.sync.dma_start(pos1_t[:], pos1)
+        nc.sync.dma_start(pos2_t[:], pos2)
+        nc.sync.dma_start(wsum_raw[:].bitcast(I32), wsum_words.rearrange("a p c -> p a c").bitcast(I32))
+        for a in range(PASSES1):
+            w1_raw[a, 1] = load_weight(w1, a, 1)
+        nc.sync.dma_start(pos3_t[:], pos3)
+        nc.sync.dma_start(gain_t[:], gain.rearrange("(b p t) -> p b t", p=P, t=PACK))
+        for b in range(PASSES2):
+            for a in range(PASSES2):
+                wd_raw[a, b] = load_weight(wdiff, a, b)
+
+        def quantize(grouped, name):
+            codes = keep.tile([P, KP], U32, name=name + "_codes", align_bytes=64)
+            scales = keep.tile([P, KP], U8, name=name + "_scales", align_bytes=64)
+            nc.vector.quantize_mx(out=codes[:].bitcast(FP8X4), scales=scales[:], in_=grouped[:])
+            return codes, scales
+
+        def prepare_weight(raw, name, vector_share=0, held=False):
+            if held:
+                grouped = keep.tile([P, PACK * KP], BF16, name="held", align_bytes=64)
+            else:
+                grouped = grp.tile([P, PACK * KP], BF16, name="grouped", align_bytes=64)
+            dst = grouped[:].rearrange("p (t m j) -> p m j t", t=PACK, j=PACK)
+            src = raw[:].rearrange("p j (m t) -> p m j t", t=PACK)
+            if vector_share:
+                nc.vector.tensor_copy(dst[:, :vector_share], src[:, :vector_share])
+            nc.scalar.copy(dst[:, vector_share:], src[:, vector_share:])
+            return quantize(grouped, name)
+
+        def gather_table(a):
+            words = keep.tile([P, S], U32, name="v_words%d" % a, align_bytes=64)
+            nc.vector.tensor_copy(words[:], tab[a][:].indirect(offs_t[:]))
+            return words
+
+        v_words = [None] * PASSES1
+        w1_q = {}
+        v_words[0] = gather_table(0)
+        w1_q[0, 0] = prepare_weight(w1_raw[0, 0], "w1_00")
+        v_sc = keep.tile([P, S], U8, name="v_sc", align_bytes=64)
+        nc.vector.tensor_copy(v_sc[:], tab_sc[:].indirect(offs_t[:]))
+        v_words[1] = gather_table(1)
+        w1_q[1, 0] = prepare_weight(w1_raw[1, 0], "w1_10")
+        v_words[2] = gather_table(2)
+
+        wsum_q = keep.tile([P, PASSES2, 2 * H], U8, name="wsum_q", align_bytes=64)
+        wsum_sc = keep.tile([P, PASSES2, H], U8, name="wsum_sc", align_bytes=64)
+        nc.vector.tensor_copy(
+            wsum_sc[:].rearrange("p a (b t m) -> p (a b) m t", t=PACK, m=P),
+            wsum_sc_raw[:].rearrange("p a (b m t) -> p (a b) m t", t=PACK, m=P),
+        )
+        w1_q[2, 0] = prepare_weight(w1_raw[2, 0], "w1_20", VECTOR_SHARE)
+        nc.vector.tensor_copy(
+            wsum_q[:].bitcast(U16).rearrange("p a (b t m) -> p (a b) m t", t=PACK, m=P),
+            wsum_raw[:].bitcast(U16).rearrange("p a (b m t) -> p (a b) m t", t=PACK, m=P),
+        )
+
+        h = {}
+
+        def first_stage(b):
+            banks = {}
+            for t in range(PACK):
+                for u in range(S // BANK):
+                    banks[t, u] = psum.tile([P, BANK], F32, name="bank")
+            for a in range(PASSES1):
+                codes, scales = w1_q[a, b]
+                for t in range(PACK):
+                    for u in range(S // BANK):
+                        nc.tensor.matmul_mx(
+                            out=banks[t, u][:],
+                            lhsT=codes[:, t * P : (t + 1) * P].bitcast(FP8X4),
+                            lhsT_scale=scales[:, t * P : (t + 1) * P],
+                            rhs=v_words[a][:, u * BANK : (u + 1) * BANK].bitcast(FP8X4),
+                            rhs_scale=v_sc[4 * a :, u * BANK : (u + 1) * BANK],
+                            start=(a == 0),
+                            stop=(a == PASSES1 - 1),
+                        )
+            for t in range(PACK):
+                h[b, t] = keep.tile([P, S], F32, name="h%d%d" % (b, t))
+                for u in range(S // BANK):
+                    nc.scalar.copy(h[b, t][:, u * BANK : (u + 1) * BANK], banks[t, u][:])
+
+        first_stage(0)
+        for a in range(PASSES1):
+            w1_q[a, 1] = prepare_weight(w1_raw[a, 1], "w1_%d1" % a, held=(a == PASSES1 - 1))
+        first_stage(1)
+
+        both_q = [None] * PASSES2
+        drop_q = [None] * PASSES2
+
+        def pair_up(b):
+            pair = big.tile([P, 2, PACK, SECT], F32, name="big")
+            for t in range(PACK):
+                nc.vector.tensor_copy(pair[:, 0, t, :], h[b, t][:].indirect(pos1_t[:]))
+                nc.vector.tensor_copy(pair[:, 1, t, :], h[b, t][:].indirect(pos2_t[:]))
+            core = pair[:, 0].rearrange("p t (c i) -> p c t i", i=4)
+            surf = pair[:, 1].rearrange("p t (c i) -> p c t i", i=4)
+            both = keep.tile([P, PACK * SECT], BF16, name="held", align_bytes=64)
+            drop = grp.tile([P, PACK * SECT], BF16, name="grouped", align_bytes=64)
+            nc.vector.tensor_tensor(both[:].rearrange("p (c i t) -> p c t i", i=4, t=PACK), core, surf, ALU.add)
+            nc.vector.tensor_tensor(drop[:].rearrange("p (c i t) -> p c t i", i=4, t=PACK), core, surf, ALU.subtract)
+            both_q[b] = quantize(both, "both%d" % b)
+            drop_q[b] = quantize(drop, "drop%d" % b)
+
+        wd_q = {}
+        pair_up(0)
+        for b in range(PASSES2):
+            for a in range(PASSES2):
+                wd_q[a, b] = prepare_weight(wd_raw[a, b], "wd_%d%d" % (a, b))
+
+        def scale_by_gain(b, t):
+            nc.scalar.activation(h[b, t][:], h[b, t][:], ACT.Copy, scale=gain_t[:, b, t : t + 1])
+
+        for t in range(PACK):
+            scale_by_gain(0, t)
+        pair_up(1)
+
+        def second_stage(b, t, y):
+            c0 = b * KP + t * P
+            level = psum.tile([P, BANK], F32, name="bank")
+            grad = psum.tile([P, BANK], F32, name="bank")
+            for a in range(PASSES2):
+                nc.tensor.matmul_mx(
+                    out=level[:],
+                    lhsT=wsum_q[:, a, 2 * c0 : 2 * (c0 + P)].bitcast(FP4X4),
+                    lhsT_scale=wsum_sc[:, a, c0 : c0 + P],
+                    rhs=both_q[a][0][:].bitcast(FP8X4),
+                    rhs_scale=both_q[a][1][:],
+                    start=(a == 0),
+                    stop=(a == PASSES2 - 1),
+                )
+            for a in range(PASSES2):
+                codes, scales = wd_q[a, b]
+                nc.tensor.matmul_mx(
+                    out=grad[:],
+                    lhsT=codes[:, t * P : (t + 1) * P].bitcast(FP8X4),
+                    lhsT_scale=scales[:, t * P : (t + 1) * P],
+                    rhs=drop_q[a][0][:].bitcast(FP8X4),
+                    rhs_scale=drop_q[a][1][:],
+                    start=(a == 0),
+                    stop=(a == PASSES2 - 1),
+                )
+            nc.scalar.copy(y, level[:])
+            nc.vector.tensor_tensor(y, grad[:], y, ALU.max)
+
+        out_rows = out.rearrange("(b p t) j -> b t p j", p=P, t=PACK)
+        order = [(b, t) for b in range(PASSES2) for t in range(PACK)]
+        first_y = rawp.tile([P, SECT], F32, name="raw")
+        y = first_y[:]
+        second_stage(*order[0], y)
+        for n, (b, t) in enumerate(order):
+            last = n == len(order) - 1
+            window = big.tile([P, (2 if last else 3) * SECT], F32, name="big")
+            logs = window[:, :SECT]
+            square = window[:, SECT : 2 * SECT]
+            nc.scalar.activation(square, y, ACT.Square)
+            nc.scalar.activation(logs, square, ACT.Ln, bias=1.0)
+            if not last:
+                y = window[:, 2 * SECT :]
+                second_stage(*order[n + 1], y)
+            if b == 0:
+                scale_by_gain(1, t)
+            result = rawp.tile([P, S], F32, name="raw")
+            pieces = 2 if last else 1
+            width = S // pieces
+            for i in range(pieces):
+                cols = slice(i * width, (i + 1) * width)
+                entries = pos3_t[:, i * width // 16 : (i + 1) * width // 16]
+                nc.vector.tensor_tensor(result[:, cols], window[:].indirect(entries), h[b, t][:, cols], ALU.add)
+                nc.sync.dma_start(out_rows[b, t][:, cols], result[:, cols])

@@ -23,6 +23,7 @@ BANK = 512
 PASSES1 = K // KP
 PASSES2 = H // KP
 VECTOR_SHARE = 84
+GAIN_LEAD = 2
 
 
 def tile_list_curing_crack_score_kernel(
@@ -32,9 +33,10 @@ def tile_list_curing_crack_score_kernel(
     with ExitStack() as ctx:
         keep = ctx.enter_context(tc.tile_pool(name="keep", bufs=1))
         big = ctx.enter_context(tc.tile_pool(name="big", bufs=3))
-        rawp = ctx.enter_context(tc.tile_pool(name="rawp", bufs=8))
-        grp = ctx.enter_context(tc.tile_pool(name="grp", bufs=3))
-        psum = ctx.enter_context(tc.psum_pool(name="psum", bufs=8))
+        rawp = ctx.enter_context(tc.tile_pool(name="rawp", bufs=6))
+        grp = ctx.enter_context(tc.tile_pool(name="grp", bufs=6))
+        psum = ctx.enter_context(tc.psum_pool(name="psum", bufs=1))
+        banks = [psum.tile([P, BANK], F32, name="bank%d" % i) for i in range(8)]
 
         offs_t = keep.tile([P, S // 16], U16, name="offs_t")
         pos1_t = keep.tile([P, SECT // 16], U16, name="pos1_t")
@@ -82,22 +84,30 @@ def tile_list_curing_crack_score_kernel(
         w1_raw[2, 0] = load_weight(w1, 2, 0)
         nc.sync.dma_start(pos1_t[:], pos1)
         nc.sync.dma_start(pos2_t[:], pos2)
+        nc.sync.dma_start(pos3_t[:], pos3)
+        nc.sync.dma_start(gain_t[:], gain.rearrange("(b p t) -> p b t", p=P, t=PACK))
         nc.sync.dma_start(wsum_raw[:].bitcast(I32), wsum_words.rearrange("a p c -> p a c").bitcast(I32))
         for a in range(PASSES1):
             w1_raw[a, 1] = load_weight(w1, a, 1)
-        nc.sync.dma_start(pos3_t[:], pos3)
-        nc.sync.dma_start(gain_t[:], gain.rearrange("(b p t) -> p b t", p=P, t=PACK))
         for b in range(PASSES2):
             for a in range(PASSES2):
                 wd_raw[a, b] = load_weight(wdiff, a, b)
 
-        def quantize(grouped, name):
-            codes = keep.tile([P, KP], U32, name=name + "_codes", align_bytes=64)
+        def quantize(grouped, name, widths=(KP,), codes=None):
+            if codes is None:
+                codes = keep.tile([P, KP], U32, name=name + "_codes", align_bytes=64)
             scales = keep.tile([P, KP], U8, name=name + "_scales", align_bytes=64)
-            nc.vector.quantize_mx(out=codes[:].bitcast(FP8X4), scales=scales[:], in_=grouped[:])
+            c0 = 0
+            for width in widths:
+                nc.vector.quantize_mx(
+                    out=codes[:, c0 : c0 + width].bitcast(FP8X4),
+                    scales=scales[:, c0 : c0 + width],
+                    in_=grouped[:, PACK * c0 : PACK * (c0 + width)],
+                )
+                c0 = c0 + width
             return codes, scales
 
-        def prepare_weight(raw, name, vector_share=0, held=False):
+        def prepare_weight(raw, name, vector_share=0, held=False, defer=False):
             if held:
                 grouped = keep.tile([P, PACK * KP], BF16, name="held", align_bytes=64)
             else:
@@ -107,7 +117,9 @@ def tile_list_curing_crack_score_kernel(
             if vector_share:
                 nc.vector.tensor_copy(dst[:, :vector_share], src[:, :vector_share])
             nc.scalar.copy(dst[:, vector_share:], src[:, vector_share:])
-            return quantize(grouped, name)
+            if defer:
+                return grouped
+            return quantize(grouped, name, (P, P, 2 * P) if vector_share else (KP,))
 
         def gather_table(a):
             words = keep.tile([P, S], U32, name="v_words%d" % a, align_bytes=64)
@@ -139,16 +151,12 @@ def tile_list_curing_crack_score_kernel(
         h = {}
 
         def first_stage(b):
-            banks = {}
-            for t in range(PACK):
-                for u in range(S // BANK):
-                    banks[t, u] = psum.tile([P, BANK], F32, name="bank")
             for a in range(PASSES1):
                 codes, scales = w1_q[a, b]
                 for t in range(PACK):
                     for u in range(S // BANK):
                         nc.tensor.matmul_mx(
-                            out=banks[t, u][:],
+                            out=banks[2 * t + u][:],
                             lhsT=codes[:, t * P : (t + 1) * P].bitcast(FP8X4),
                             lhsT_scale=scales[:, t * P : (t + 1) * P],
                             rhs=v_words[a][:, u * BANK : (u + 1) * BANK].bitcast(FP8X4),
@@ -159,7 +167,10 @@ def tile_list_curing_crack_score_kernel(
             for t in range(PACK):
                 h[b, t] = keep.tile([P, S], F32, name="h%d%d" % (b, t))
                 for u in range(S // BANK):
-                    nc.scalar.copy(h[b, t][:, u * BANK : (u + 1) * BANK], banks[t, u][:])
+                    if (b, t, u) == (0, 0, 1):
+                        nc.vector.tensor_copy(h[b, t][:, u * BANK : (u + 1) * BANK], banks[2 * t + u][:])
+                    else:
+                        nc.scalar.copy(h[b, t][:, u * BANK : (u + 1) * BANK], banks[2 * t + u][:])
 
         first_stage(0)
         for a in range(PASSES1):
@@ -172,34 +183,54 @@ def tile_list_curing_crack_score_kernel(
         def pair_up(b):
             pair = big.tile([P, 2, PACK, SECT], F32, name="big")
             for t in range(PACK):
-                nc.vector.tensor_copy(pair[:, 0, t, :], h[b, t][:].indirect(pos1_t[:]))
-                nc.vector.tensor_copy(pair[:, 1, t, :], h[b, t][:].indirect(pos2_t[:]))
-            core = pair[:, 0].rearrange("p t (c i) -> p c t i", i=4)
-            surf = pair[:, 1].rearrange("p t (c i) -> p c t i", i=4)
+                nc.vector.tensor_copy(pair[:, 0, t, :], h[b, t][:].indirect(pos2_t[:]))
+            for t in range(PACK):
+                nc.vector.tensor_tensor(
+                    pair[:, 1, t, :], h[b, t][:].indirect(pos1_t[:]), pair[:, 0, t, :], ALU.subtract
+                )
             both = keep.tile([P, PACK * SECT], BF16, name="held", align_bytes=64)
-            drop = grp.tile([P, PACK * SECT], BF16, name="grouped", align_bytes=64)
-            nc.vector.tensor_tensor(both[:].rearrange("p (c i t) -> p c t i", i=4, t=PACK), core, surf, ALU.add)
-            nc.vector.tensor_tensor(drop[:].rearrange("p (c i t) -> p c t i", i=4, t=PACK), core, surf, ALU.subtract)
+            drop = keep.tile([P, PACK * SECT], BF16, name="late", align_bytes=64)
+            nc.scalar.copy(
+                drop[:].rearrange("p (c i t) -> p c t i", i=4, t=PACK),
+                pair[:, 1].rearrange("p t (c i) -> p c t i", i=4),
+            )
+            nc.vector.scalar_tensor_tensor(
+                both[:].rearrange("p (m t) -> p m t", t=PACK),
+                pair[:, 0].rearrange("p t m -> p m t"),
+                2.0,
+                pair[:, 1].rearrange("p t m -> p m t"),
+                ALU.mult,
+                ALU.add,
+            )
             both_q[b] = quantize(both, "both%d" % b)
             drop_q[b] = quantize(drop, "drop%d" % b)
 
         wd_q = {}
         pair_up(0)
-        for b in range(PASSES2):
-            for a in range(PASSES2):
-                wd_q[a, b] = prepare_weight(wd_raw[a, b], "wd_%d%d" % (a, b))
+        for a in range(PASSES2):
+            wd_q[a, 0] = prepare_weight(wd_raw[a, 0], "wd_%d0" % a)
+        wd_grouped = [prepare_weight(wd_raw[a, 1], "wd_%d1" % a, defer=True) for a in range(PASSES2)]
 
-        def scale_by_gain(b, t):
-            nc.scalar.activation(h[b, t][:], h[b, t][:], ACT.Copy, scale=gain_t[:, b, t : t + 1])
+        order = [(b, t) for b in range(PASSES2) for t in range(PACK)]
+        rows = {}
 
-        for t in range(PACK):
-            scale_by_gain(0, t)
+        def scale_by_gain(n):
+            b, t = order[n]
+            nc.scalar.activation(rows[n][:, :S], h[b, t][:], ACT.Copy, scale=gain_t[:, b, t : t + 1])
+
+        for n in range(GAIN_LEAD):
+            rows[n] = rawp.tile([P, 2 * S], F32, name="raw")
+            scale_by_gain(n)
         pair_up(1)
+        late_codes = keep.tile([P, PASSES2 * KP], U32, name="late", align_bytes=64)
+        for a in range(PASSES2):
+            wd_q[a, 1] = quantize(wd_grouped[a], "wd_%d1" % a, codes=late_codes[:, a * KP : (a + 1) * KP])
 
-        def second_stage(b, t, y):
+        def second_stage(n, y, level_sb):
+            b, t = order[n]
             c0 = b * KP + t * P
-            level = psum.tile([P, BANK], F32, name="bank")
-            grad = psum.tile([P, BANK], F32, name="bank")
+            level = banks[n % 2]
+            grad = banks[2 + n % 2]
             for a in range(PASSES2):
                 nc.tensor.matmul_mx(
                     out=level[:],
@@ -221,31 +252,35 @@ def tile_list_curing_crack_score_kernel(
                     start=(a == 0),
                     stop=(a == PASSES2 - 1),
                 )
-            nc.scalar.copy(y, level[:])
-            nc.vector.tensor_tensor(y, grad[:], y, ALU.max)
+            nc.scalar.copy(level_sb, level[:])
+            nc.vector.tensor_tensor(y, grad[:], level_sb, ALU.max)
 
         out_rows = out.rearrange("(b p t) j -> b t p j", p=P, t=PACK)
-        order = [(b, t) for b in range(PASSES2) for t in range(PACK)]
-        first_y = rawp.tile([P, SECT], F32, name="raw")
-        y = first_y[:]
-        second_stage(*order[0], y)
+        first = rawp.tile([P, 2 * SECT], F32, name="raw")
+        y = first[:, :SECT]
+        second_stage(0, y, first[:, SECT:])
         for n, (b, t) in enumerate(order):
             last = n == len(order) - 1
             window = big.tile([P, (2 if last else 3) * SECT], F32, name="big")
             logs = window[:, :SECT]
-            square = window[:, SECT : 2 * SECT]
+            if last:
+                square = window[:, SECT:]
+            else:
+                rows[n + GAIN_LEAD] = rawp.tile([P, 2 * S], F32, name="raw")
+                square = rows[n + GAIN_LEAD][:, :SECT]
             nc.scalar.activation(square, y, ACT.Square)
             nc.scalar.activation(logs, square, ACT.Ln, bias=1.0)
             if not last:
-                y = window[:, 2 * SECT :]
-                second_stage(*order[n + 1], y)
-            if b == 0:
-                scale_by_gain(1, t)
-            result = rawp.tile([P, S], F32, name="raw")
+                y = window[:, SECT : 2 * SECT]
+                second_stage(n + 1, y, window[:, 2 * SECT :])
+            if n + GAIN_LEAD < len(order):
+                scale_by_gain(n + GAIN_LEAD)
+            gained = rows[n][:, :S]
+            result = rows[n][:, S:]
             pieces = 2 if last else 1
             width = S // pieces
             for i in range(pieces):
                 cols = slice(i * width, (i + 1) * width)
                 entries = pos3_t[:, i * width // 16 : (i + 1) * width // 16]
-                nc.vector.tensor_tensor(result[:, cols], window[:].indirect(entries), h[b, t][:, cols], ALU.add)
+                nc.vector.tensor_tensor(result[:, cols], window[:].indirect(entries), gained[:, cols], ALU.add)
                 nc.sync.dma_start(out_rows[b, t][:, cols], result[:, cols])

@@ -23,7 +23,8 @@ BANK = 512
 PASSES1 = K // KP
 PASSES2 = H // KP
 VECTOR_SHARE = 84
-GAIN_LEAD = 2
+RING = 4
+SPARE = 16
 
 
 def tile_list_curing_crack_score_kernel(
@@ -34,7 +35,7 @@ def tile_list_curing_crack_score_kernel(
         keep = ctx.enter_context(tc.tile_pool(name="keep", bufs=1))
         big = ctx.enter_context(tc.tile_pool(name="big", bufs=3))
         rawp = ctx.enter_context(tc.tile_pool(name="rawp", bufs=6))
-        grp = ctx.enter_context(tc.tile_pool(name="grp", bufs=6))
+        grp = ctx.enter_context(tc.tile_pool(name="grp", bufs=4))
         psum = ctx.enter_context(tc.psum_pool(name="psum", bufs=1))
         banks = [psum.tile([P, BANK], F32, name="bank%d" % i) for i in range(8)]
 
@@ -47,11 +48,21 @@ def tile_list_curing_crack_score_kernel(
         wsum_raw = keep.tile([P, PASSES2, 2 * H], U8, name="wsum_raw")
         wsum_sc_raw = keep.tile([P, PASSES2, H], U8, name="wsum_sc_raw")
 
-        nc.vector.memset(tab_sc[:].bitcast(I32), 0)
+        nc.gpsimd.memset(tab_sc[:].bitcast(I32), 0)
+        for q in range(4):
+            nc.gpsimd.dma_start(
+                tab_sc[32 * q : 32 * q + 4 * PASSES1, :].bitcast(I32),
+                tab_scales[:, 4 * q : 4 * q + 4, :].bitcast(I32),
+            )
         nc.vector.memset(wsum_sc_raw[:].bitcast(I32), 0)
+        for q in range(4):
+            nc.gpsimd.dma_start(
+                wsum_sc_raw[32 * q : 32 * q + 4, :, :].bitcast(I32),
+                wsum_scales[:, 4 * q : 4 * q + 4, :].rearrange("a r c -> r a c").bitcast(I32),
+            )
 
         def load_table(a):
-            words = big.tile([P, T], U32, name="big")
+            words = big.tile([P, T], U32, name="big", align_bytes=64)
             nc.sync.dma_start(words[:].bitcast(I32), tab_words[a].rearrange("p t i -> p (t i)").bitcast(I32))
             return words
 
@@ -67,31 +78,27 @@ def tile_list_curing_crack_score_kernel(
         wd_raw = {}
         nc.sync.dma_start(offs_t[:], offs)
         tab[0] = load_table(0)
-        for q in range(4):
-            nc.sync.dma_start(
-                tab_sc[32 * q : 32 * q + 4 * PASSES1, :].bitcast(I32),
-                tab_scales[:, 4 * q : 4 * q + 4, :].bitcast(I32),
-            )
-        w1_raw[0, 0] = load_weight(w1, 0, 0)
-        tab[1] = load_table(1)
-        w1_raw[1, 0] = load_weight(w1, 1, 0)
-        for q in range(4):
-            nc.sync.dma_start(
-                wsum_sc_raw[32 * q : 32 * q + 4, :, :].bitcast(I32),
-                wsum_scales[:, 4 * q : 4 * q + 4, :].rearrange("a r c -> r a c").bitcast(I32),
-            )
-        tab[2] = load_table(2)
-        w1_raw[2, 0] = load_weight(w1, 2, 0)
         nc.sync.dma_start(pos1_t[:], pos1)
         nc.sync.dma_start(pos2_t[:], pos2)
         nc.sync.dma_start(pos3_t[:], pos3)
         nc.sync.dma_start(gain_t[:], gain.rearrange("(b p t) -> p b t", p=P, t=PACK))
+        w1_raw[0, 0] = load_weight(w1, 0, 0)
+        for a in range(1, PASSES1):
+            tab[a] = load_table(a)
+            w1_raw[a, 0] = load_weight(w1, a, 0)
         nc.sync.dma_start(wsum_raw[:].bitcast(I32), wsum_words.rearrange("a p c -> p a c").bitcast(I32))
         for a in range(PASSES1):
             w1_raw[a, 1] = load_weight(w1, a, 1)
         for b in range(PASSES2):
             for a in range(PASSES2):
                 wd_raw[a, b] = load_weight(wdiff, a, b)
+
+        warm = keep.tile([P, 2], F32, name="warm")
+        nc.vector.memset(warm[:, 0:1], 0.0)
+        nc.scalar.activation(warm[:, 1:2], warm[:, 0:1], ACT.Ln, bias=1.0)
+        windows = [keep.tile([P, S + SPARE], F32, name="window%d" % i) for i in range(RING)]
+        for window in windows:
+            nc.vector.memset(window[:, S:], 0.0)
 
         def quantize(grouped, name, widths=(KP,), codes=None):
             if codes is None:
@@ -107,18 +114,17 @@ def tile_list_curing_crack_score_kernel(
                 c0 = c0 + width
             return codes, scales
 
-        def prepare_weight(raw, name, vector_share=0, held=False, defer=False):
-            if held:
-                grouped = keep.tile([P, PACK * KP], BF16, name="held", align_bytes=64)
-            else:
-                grouped = grp.tile([P, PACK * KP], BF16, name="grouped", align_bytes=64)
-            dst = grouped[:].rearrange("p (t m j) -> p m j t", t=PACK, j=PACK)
+        def interleave_weight(raw, grouped, vector_share=0):
+            dst = grouped.rearrange("p (t m j) -> p m j t", t=PACK, j=PACK)
             src = raw[:].rearrange("p j (m t) -> p m j t", t=PACK)
             if vector_share:
                 nc.vector.tensor_copy(dst[:, :vector_share], src[:, :vector_share])
             nc.scalar.copy(dst[:, vector_share:], src[:, vector_share:])
-            if defer:
-                return grouped
+
+        def prepare_weight(raw, name, vector_share=0, grouped=None):
+            if grouped is None:
+                grouped = grp.tile([P, PACK * KP], BF16, name="grouped", align_bytes=64)[:]
+            interleave_weight(raw, grouped, vector_share)
             return quantize(grouped, name, (P, P, 2 * P) if vector_share else (KP,))
 
         def gather_table(a):
@@ -143,10 +149,11 @@ def tile_list_curing_crack_score_kernel(
             wsum_sc_raw[:].rearrange("p a (b m t) -> p (a b) m t", t=PACK, m=P),
         )
         w1_q[2, 0] = prepare_weight(w1_raw[2, 0], "w1_20", VECTOR_SHARE)
-        nc.vector.tensor_copy(
-            wsum_q[:].bitcast(U16).rearrange("p a (b t m) -> p (a b) m t", t=PACK, m=P),
-            wsum_raw[:].bitcast(U16).rearrange("p a (b m t) -> p (a b) m t", t=PACK, m=P),
-        )
+        for a in range(PASSES2):
+            nc.vector.tensor_copy(
+                wsum_q[:, a].bitcast(U16).rearrange("p (b t m) -> p b m t", t=PACK, m=P),
+                wsum_raw[:, a].bitcast(U16).rearrange("p (b m t) -> p b m t", t=PACK, m=P),
+            )
 
         h = {}
 
@@ -173,60 +180,52 @@ def tile_list_curing_crack_score_kernel(
                         nc.scalar.copy(h[b, t][:, u * BANK : (u + 1) * BANK], banks[2 * t + u][:])
 
         first_stage(0)
+        pairs = [big.tile([P, 2 * PACK * SECT], F32, name="big", align_bytes=64) for b in range(PASSES2)]
+        held = keep.tile([P, PACK * KP], BF16, name="held", align_bytes=64)
+        staging = [pairs[0][:, 2 * t * SECT : 2 * (t + 1) * SECT].bitcast(BF16) for t in (2, 3)] + [held[:]]
         for a in range(PASSES1):
-            w1_q[a, 1] = prepare_weight(w1_raw[a, 1], "w1_%d1" % a, held=(a == PASSES1 - 1))
+            w1_q[a, 1] = prepare_weight(w1_raw[a, 1], "w1_%d1" % a, grouped=staging[a])
         first_stage(1)
 
         both_q = [None] * PASSES2
         drop_q = [None] * PASSES2
 
         def pair_up(b):
-            pair = big.tile([P, 2, PACK, SECT], F32, name="big")
+            pair = pairs[b][:].rearrange("p (t s m) -> p s t m", t=PACK, s=2)
             for t in range(PACK):
-                nc.vector.tensor_copy(pair[:, 0, t, :], h[b, t][:].indirect(pos2_t[:]))
-            for t in range(PACK):
-                nc.vector.tensor_tensor(
-                    pair[:, 1, t, :], h[b, t][:].indirect(pos1_t[:]), pair[:, 0, t, :], ALU.subtract
-                )
+                nc.vector.tensor_copy(pair[:, 0, t, :], h[b, t][:].indirect(pos1_t[:]))
+                nc.vector.tensor_copy(pair[:, 1, t, :], h[b, t][:].indirect(pos2_t[:]))
+            core = pair[:, 0].rearrange("p t (c i) -> p c t i", i=4)
+            surf = pair[:, 1].rearrange("p t (c i) -> p c t i", i=4)
             both = keep.tile([P, PACK * SECT], BF16, name="held", align_bytes=64)
             drop = keep.tile([P, PACK * SECT], BF16, name="late", align_bytes=64)
-            nc.scalar.copy(
-                drop[:].rearrange("p (c i t) -> p c t i", i=4, t=PACK),
-                pair[:, 1].rearrange("p t (c i) -> p c t i", i=4),
-            )
-            nc.vector.scalar_tensor_tensor(
-                both[:].rearrange("p (m t) -> p m t", t=PACK),
-                pair[:, 0].rearrange("p t m -> p m t"),
-                2.0,
-                pair[:, 1].rearrange("p t m -> p m t"),
-                ALU.mult,
-                ALU.add,
-            )
-            both_q[b] = quantize(both, "both%d" % b)
-            drop_q[b] = quantize(drop, "drop%d" % b)
+            nc.vector.tensor_tensor(both[:].rearrange("p (c i t) -> p c t i", i=4, t=PACK), core, surf, ALU.add)
+            nc.vector.tensor_tensor(drop[:].rearrange("p (c i t) -> p c t i", i=4, t=PACK), core, surf, ALU.subtract)
+            both_q[b] = quantize(both[:], "both%d" % b)
+            drop_q[b] = quantize(drop[:], "drop%d" % b)
+
+        def scale_by_gain(b, t):
+            nc.scalar.activation(h[b, t][:], h[b, t][:], ACT.Copy, scale=gain_t[:, b, t : t + 1])
 
         wd_q = {}
         pair_up(0)
         for a in range(PASSES2):
             wd_q[a, 0] = prepare_weight(wd_raw[a, 0], "wd_%d0" % a)
-        wd_grouped = [prepare_weight(wd_raw[a, 1], "wd_%d1" % a, defer=True) for a in range(PASSES2)]
-
-        order = [(b, t) for b in range(PASSES2) for t in range(PACK)]
-        rows = {}
-
-        def scale_by_gain(n):
-            b, t = order[n]
-            nc.scalar.activation(rows[n][:, :S], h[b, t][:], ACT.Copy, scale=gain_t[:, b, t : t + 1])
-
-        for n in range(GAIN_LEAD):
-            rows[n] = rawp.tile([P, 2 * S], F32, name="raw")
-            scale_by_gain(n)
+        wd_grouped = [grp.tile([P, PACK * KP], BF16, name="grouped", align_bytes=64) for a in range(PASSES2)]
+        for a in range(PASSES2):
+            interleave_weight(wd_raw[a, 1], wd_grouped[a][:])
+        for t in range(PACK):
+            scale_by_gain(0, t)
         pair_up(1)
+        for t in range(PACK):
+            scale_by_gain(1, t)
         late_codes = keep.tile([P, PASSES2 * KP], U32, name="late", align_bytes=64)
         for a in range(PASSES2):
-            wd_q[a, 1] = quantize(wd_grouped[a], "wd_%d1" % a, codes=late_codes[:, a * KP : (a + 1) * KP])
+            wd_q[a, 1] = quantize(wd_grouped[a][:], "wd_%d1" % a, codes=late_codes[:, a * KP : (a + 1) * KP])
 
-        def second_stage(n, y, level_sb):
+        order = [(b, t) for b in range(PASSES2) for t in range(PACK)]
+
+        def second_stage(n):
             b, t = order[n]
             c0 = b * KP + t * P
             level = banks[n % 2]
@@ -252,35 +251,24 @@ def tile_list_curing_crack_score_kernel(
                     start=(a == 0),
                     stop=(a == PASSES2 - 1),
                 )
-            nc.scalar.copy(level_sb, level[:])
-            nc.vector.tensor_tensor(y, grad[:], level_sb, ALU.max)
+            y = windows[n % RING][:, SECT : 2 * SECT]
+            nc.scalar.copy(y, level[:])
+            nc.vector.tensor_tensor(y, grad[:], y, ALU.max)
 
         out_rows = out.rearrange("(b p t) j -> b t p j", p=P, t=PACK)
-        first = rawp.tile([P, 2 * SECT], F32, name="raw")
-        y = first[:, :SECT]
-        second_stage(0, y, first[:, SECT:])
+        second_stage(0)
         for n, (b, t) in enumerate(order):
             last = n == len(order) - 1
-            window = big.tile([P, (2 if last else 3) * SECT], F32, name="big")
-            logs = window[:, :SECT]
-            if last:
-                square = window[:, SECT:]
-            else:
-                rows[n + GAIN_LEAD] = rawp.tile([P, 2 * S], F32, name="raw")
-                square = rows[n + GAIN_LEAD][:, :SECT]
-            nc.scalar.activation(square, y, ACT.Square)
-            nc.scalar.activation(logs, square, ACT.Ln, bias=1.0)
             if not last:
-                y = window[:, SECT : 2 * SECT]
-                second_stage(n + 1, y, window[:, 2 * SECT :])
-            if n + GAIN_LEAD < len(order):
-                scale_by_gain(n + GAIN_LEAD)
-            gained = rows[n][:, :S]
-            result = rows[n][:, S:]
-            pieces = 2 if last else 1
-            width = S // pieces
-            for i in range(pieces):
-                cols = slice(i * width, (i + 1) * width)
-                entries = pos3_t[:, i * width // 16 : (i + 1) * width // 16]
-                nc.vector.tensor_tensor(result[:, cols], window[:].indirect(entries), gained[:, cols], ALU.add)
+                second_stage(n + 1)
+            window = windows[n % RING]
+            square = keep.tile([P, SECT], F32, name="square")
+            nc.scalar.activation(square[:], window[:, SECT : 2 * SECT], ACT.Square)
+            nc.scalar.activation(window[:, :SECT], square[:], ACT.Ln, bias=1.0)
+            result = rawp.tile([P, S], F32, name="raw")
+            edges = (0, S // 2, 3 * S // 4, S) if last else (0, S)
+            for c0, c1 in zip(edges, edges[1:]):
+                cols = slice(c0, c1)
+                entries = pos3_t[:, c0 // 16 : c1 // 16]
+                nc.vector.tensor_tensor(result[:, cols], window[:].indirect(entries), h[b, t][:, cols], ALU.add)
                 nc.sync.dma_start(out_rows[b, t][:, cols], result[:, cols])

@@ -115,17 +115,18 @@ def tile_list_curing_crack_score_kernel(
             return codes, scales
 
         def interleave_weight(raw, grouped, vector_share=0):
-            dst = grouped.rearrange("p (t m j) -> p m j t", t=PACK, j=PACK)
-            src = raw[:].rearrange("p j (m t) -> p m j t", t=PACK)
-            if vector_share:
-                nc.vector.tensor_copy(dst[:, :vector_share], src[:, :vector_share])
-            nc.scalar.copy(dst[:, vector_share:], src[:, vector_share:])
+            dst = grouped.rearrange("p (u e m j) -> p u m j e", u=2, e=2, j=PACK)
+            src = raw[:].rearrange("p j (m u e) -> p u m j e", u=2, e=2)
+            for u in range(2):
+                if vector_share:
+                    nc.vector.tensor_copy(dst[:, u, :vector_share], src[:, u, :vector_share])
+                nc.scalar.copy(dst[:, u, vector_share:], src[:, u, vector_share:])
 
         def prepare_weight(raw, name, vector_share=0, grouped=None):
             if grouped is None:
                 grouped = grp.tile([P, PACK * KP], BF16, name="grouped", align_bytes=64)[:]
             interleave_weight(raw, grouped, vector_share)
-            return quantize(grouped, name, (P, P, 2 * P) if vector_share else (KP,))
+            return quantize(grouped, name, (2 * P, 2 * P) if vector_share else (KP,))
 
         def gather_table(a):
             words = keep.tile([P, S], U32, name="v_words%d" % a, align_bytes=64)
@@ -145,14 +146,14 @@ def tile_list_curing_crack_score_kernel(
         wsum_q = keep.tile([P, PASSES2, 2 * H], U8, name="wsum_q", align_bytes=64)
         wsum_sc = keep.tile([P, PASSES2, H], U8, name="wsum_sc", align_bytes=64)
         nc.vector.tensor_copy(
-            wsum_sc[:].rearrange("p a (b t m) -> p (a b) m t", t=PACK, m=P),
-            wsum_sc_raw[:].rearrange("p a (b m t) -> p (a b) m t", t=PACK, m=P),
+            wsum_sc[:].rearrange("p a (b t m) -> p (a b) t m", t=PACK, m=P),
+            wsum_sc_raw[:].rearrange("p a (b m t) -> p (a b) t m", t=PACK, m=P),
         )
         w1_q[2, 0] = prepare_weight(w1_raw[2, 0], "w1_20", VECTOR_SHARE)
         for a in range(PASSES2):
             nc.vector.tensor_copy(
-                wsum_q[:, a].bitcast(U16).rearrange("p (b t m) -> p b m t", t=PACK, m=P),
-                wsum_raw[:, a].bitcast(U16).rearrange("p (b m t) -> p b m t", t=PACK, m=P),
+                wsum_q[:, a].bitcast(U16).rearrange("p (b t m) -> p b t m", t=PACK, m=P),
+                wsum_raw[:, a].bitcast(U16).rearrange("p (b m t) -> p b t m", t=PACK, m=P),
             )
 
         h = {}
@@ -182,7 +183,8 @@ def tile_list_curing_crack_score_kernel(
         first_stage(0)
         pairs = [big.tile([P, 2 * PACK * SECT], F32, name="big", align_bytes=64) for b in range(PASSES2)]
         held = keep.tile([P, PACK * KP], BF16, name="held", align_bytes=64)
-        staging = [pairs[0][:, 2 * t * SECT : 2 * (t + 1) * SECT].bitcast(BF16) for t in (2, 3)] + [held[:]]
+        late = keep.tile([P, PACK * KP], BF16, name="late", align_bytes=64)
+        staging = [pairs[0][:, 5 * SECT : 7 * SECT].bitcast(BF16), held[:], late[:]]
         for a in range(PASSES1):
             w1_q[a, 1] = prepare_weight(w1_raw[a, 1], "w1_%d1" % a, grouped=staging[a])
         first_stage(1)
@@ -195,12 +197,12 @@ def tile_list_curing_crack_score_kernel(
             for t in range(PACK):
                 nc.vector.tensor_copy(pair[:, 0, t, :], h[b, t][:].indirect(pos1_t[:]))
                 nc.vector.tensor_copy(pair[:, 1, t, :], h[b, t][:].indirect(pos2_t[:]))
-            core = pair[:, 0].rearrange("p t (c i) -> p c t i", i=4)
-            surf = pair[:, 1].rearrange("p t (c i) -> p c t i", i=4)
+            core = pair[:, 0].rearrange("p t (c i) -> p c t i", i=2)
+            surf = pair[:, 1].rearrange("p t (c i) -> p c t i", i=2)
             both = keep.tile([P, PACK * SECT], BF16, name="held", align_bytes=64)
             drop = keep.tile([P, PACK * SECT], BF16, name="late", align_bytes=64)
-            nc.vector.tensor_tensor(both[:].rearrange("p (c i t) -> p c t i", i=4, t=PACK), core, surf, ALU.add)
-            nc.vector.tensor_tensor(drop[:].rearrange("p (c i t) -> p c t i", i=4, t=PACK), core, surf, ALU.subtract)
+            nc.vector.tensor_tensor(both[:].rearrange("p (c i t) -> p c t i", i=2, t=PACK), core, surf, ALU.add)
+            nc.vector.tensor_tensor(drop[:].rearrange("p (c i t) -> p c t i", i=2, t=PACK), core, surf, ALU.subtract)
             both_q[b] = quantize(both[:], "both%d" % b)
             drop_q[b] = quantize(drop[:], "drop%d" % b)
 

from contextlib import ExitStack

import concourse.mybir as mybir

K, H, T, S, SECT = 1536, 1024, 4096, 1024, 512
FLOPS = 2 * K * H * S + 2 * 2 * H * H * SECT

F32 = mybir.dt.float32
BF16 = mybir.dt.bfloat16
I32 = mybir.dt.int32
U32 = mybir.dt.uint32
U16 = mybir.dt.uint16
U8 = mybir.dt.uint8
FP8X4 = mybir.dt.float8_e4m3fn_x4
FP4X4 = mybir.dt.float4_e2m1fn_x4
ALU = mybir.AluOpType
ACT = mybir.ActivationFunctionType

P = 128
PACK = 4
KP = P * PACK
BANK = 512
PASSES1 = K // KP
PASSES2 = H // KP
VECTOR_SHARE = 84
RING = 4
SPARE = 16


def tile_list_curing_crack_score_kernel(
    tc, tab_words, tab_scales, offs, pos1, pos2, pos3, w1, wsum_words, wsum_scales, wdiff, gain, out
):
    nc = tc.nc
    with ExitStack() as ctx:
        keep = ctx.enter_context(tc.tile_pool(name="keep", bufs=1))
        big = ctx.enter_context(tc.tile_pool(name="big", bufs=3))
        rawp = ctx.enter_context(tc.tile_pool(name="rawp", bufs=6))
        grp = ctx.enter_context(tc.tile_pool(name="grp", bufs=4))
        psum = ctx.enter_context(tc.psum_pool(name="psum", bufs=1))
        banks = [psum.tile([P, BANK], F32, name="bank%d" % i) for i in range(8)]

        offs_t = keep.tile([P, S // 16], U16, name="offs_t")
        pos1_t = keep.tile([P, SECT // 16], U16, name="pos1_t")
        pos2_t = keep.tile([P, SECT // 16], U16, name="pos2_t")
        pos3_t = keep.tile([P, S // 16], U16, name="pos3_t")
        gain_t = keep.tile([P, PASSES2, PACK], F32, name="gain_t")
        tab_sc = keep.tile([P, T], U8, name="tab_sc")
        wsum_raw = keep.tile([P, PASSES2, 2 * H], U8, name="wsum_raw")
        wsum_sc_raw = keep.tile([P, PASSES2, H], U8, name="wsum_sc_raw")

        nc.gpsimd.memset(tab_sc[:].bitcast(I32), 0)
        for q in range(4):
            nc.gpsimd.dma_start(
                tab_sc[32 * q : 32 * q + 4 * PASSES1, :].bitcast(I32),
                tab_scales[:, 4 * q : 4 * q + 4, :].bitcast(I32),
            )
        nc.vector.memset(wsum_sc_raw[:].bitcast(I32), 0)
        for q in range(4):
            nc.gpsimd.dma_start(
                wsum_sc_raw[32 * q : 32 * q + 4, :, :].bitcast(I32),
                wsum_scales[:, 4 * q : 4 * q + 4, :].rearrange("a r c -> r a c").bitcast(I32),
            )

        def load_table(a):
            words = big.tile([P, T], U32, name="big", align_bytes=64)
            nc.sync.dma_start(words[:].bitcast(I32), tab_words[a].rearrange("p t i -> p (t i)").bitcast(I32))
            return words

        def load_weight(w, a, b):
            raw = rawp.tile([P, PACK, KP], F32, name="raw")
            nc.sync.dma_start(
                raw[:], w[a * KP : (a + 1) * KP, b * KP : (b + 1) * KP].rearrange("(p j) c -> p j c", j=PACK)
            )
            return raw

        tab = [None] * PASSES1
        w1_raw = {}
        wd_raw = {}
        nc.sync.dma_start(offs_t[:], offs)
        tab[0] = load_table(0)
        nc.sync.dma_start(pos1_t[:], pos1)
        nc.sync.dma_start(pos2_t[:], pos2)
        nc.sync.dma_start(pos3_t[:], pos3)
        nc.sync.dma_start(gain_t[:], gain.rearrange("(b p t) -> p b t", p=P, t=PACK))
        w1_raw[0, 0] = load_weight(w1, 0, 0)
        for a in range(1, PASSES1):
            tab[a] = load_table(a)
            w1_raw[a, 0] = load_weight(w1, a, 0)
        nc.sync.dma_start(wsum_raw[:].bitcast(I32), wsum_words.rearrange("a p c -> p a c").bitcast(I32))
        for a in range(PASSES1):
            w1_raw[a, 1] = load_weight(w1, a, 1)
        for b in range(PASSES2):
            for a in range(PASSES2):
                wd_raw[a, b] = load_weight(wdiff, a, b)

        warm = keep.tile([P, 2], F32, name="warm")
        nc.vector.memset(warm[:, 0:1], 0.0)
        nc.scalar.activation(warm[:, 1:2], warm[:, 0:1], ACT.Ln, bias=1.0)
        windows = [keep.tile([P, S + SPARE], F32, name="window%d" % i) for i in range(RING)]
        for window in windows:
            nc.vector.memset(window[:, S:], 0.0)

        def quantize(grouped, name, widths=(KP,), codes=None):
            if codes is None:
                codes = keep.tile([P, KP], U32, name=name + "_codes", align_bytes=64)
            scales = keep.tile([P, KP], U8, name=name + "_scales", align_bytes=64)
            c0 = 0
            for width in widths:
                nc.vector.quantize_mx(
                    out=codes[:, c0 : c0 + width].bitcast(FP8X4),
                    scales=scales[:, c0 : c0 + width],
                    in_=grouped[:, PACK * c0 : PACK * (c0 + width)],
                )
                c0 = c0 + width
            return codes, scales

        def interleave_weight(raw, grouped, vector_share=0):
            dst = grouped.rearrange("p (u e m j) -> p u m j e", u=2, e=2, j=PACK)
            src = raw[:].rearrange("p j (m u e) -> p u m j e", u=2, e=2)
            for u in range(2):
                if vector_share:
                    nc.vector.tensor_copy(dst[:, u, :vector_share], src[:, u, :vector_share])
                nc.scalar.copy(dst[:, u, vector_share:], src[:, u, vector_share:])

        def prepare_weight(raw, name, vector_share=0, grouped=None):
            if grouped is None:
                grouped = grp.tile([P, PACK * KP], BF16, name="grouped", align_bytes=64)[:]
            interleave_weight(raw, grouped, vector_share)
            return quantize(grouped, name, (2 * P, 2 * P) if vector_share else (KP,))

        def gather_table(a):
            words = keep.tile([P, S], U32, name="v_words%d" % a, align_bytes=64)
            nc.vector.tensor_copy(words[:], tab[a][:].indirect(offs_t[:]))
            return words

        v_words = [None] * PASSES1
        w1_q = {}
        v_words[0] = gather_table(0)
        w1_q[0, 0] = prepare_weight(w1_raw[0, 0], "w1_00")
        v_sc = keep.tile([P, S], U8, name="v_sc", align_bytes=64)
        nc.vector.tensor_copy(v_sc[:], tab_sc[:].indirect(offs_t[:]))
        v_words[1] = gather_table(1)
        w1_q[1, 0] = prepare_weight(w1_raw[1, 0], "w1_10")
        v_words[2] = gather_table(2)

        wsum_q = keep.tile([P, PASSES2, 2 * H], U8, name="wsum_q", align_bytes=64)
        wsum_sc = keep.tile([P, PASSES2, H], U8, name="wsum_sc", align_bytes=64)
        nc.vector.tensor_copy(
            wsum_sc[:].rearrange("p a (b t m) -> p (a b) t m", t=PACK, m=P),
            wsum_sc_raw[:].rearrange("p a (b m t) -> p (a b) t m", t=PACK, m=P),
        )
        w1_q[2, 0] = prepare_weight(w1_raw[2, 0], "w1_20", VECTOR_SHARE)
        for a in range(PASSES2):
            nc.vector.tensor_copy(
                wsum_q[:, a].bitcast(U16).rearrange("p (b t m) -> p b t m", t=PACK, m=P),
                wsum_raw[:, a].bitcast(U16).rearrange("p (b m t) -> p b t m", t=PACK, m=P),
            )

        h = {}

        def first_stage(b):
            for a in range(PASSES1):
                codes, scales = w1_q[a, b]
                for t in range(PACK):
                    for u in range(S // BANK):
                        nc.tensor.matmul_mx(
                            out=banks[2 * t + u][:],
                            lhsT=codes[:, t * P : (t + 1) * P].bitcast(FP8X4),
                            lhsT_scale=scales[:, t * P : (t + 1) * P],
                            rhs=v_words[a][:, u * BANK : (u + 1) * BANK].bitcast(FP8X4),
                            rhs_scale=v_sc[4 * a :, u * BANK : (u + 1) * BANK],
                            start=(a == 0),
                            stop=(a == PASSES1 - 1),
                        )
            for t in range(PACK):
                h[b, t] = keep.tile([P, S], F32, name="h%d%d" % (b, t))
                for u in range(S // BANK):
                    if (b, t, u) == (0, 0, 1):
                        nc.vector.tensor_copy(h[b, t][:, u * BANK : (u + 1) * BANK], banks[2 * t + u][:])
                    else:
                        nc.scalar.copy(h[b, t][:, u * BANK : (u + 1) * BANK], banks[2 * t + u][:])

        first_stage(0)
        pairs = [big.tile([P, 2 * PACK * SECT], F32, name="big", align_bytes=64) for b in range(PASSES2)]
        held = keep.tile([P, PACK * KP], BF16, name="held", align_bytes=64)
        late = keep.tile([P, PACK * KP], BF16, name="late", align_bytes=64)
        staging = [pairs[0][:, 5 * SECT : 7 * SECT].bitcast(BF16), held[:], late[:]]
        for a in range(PASSES1):
            w1_q[a, 1] = prepare_weight(w1_raw[a, 1], "w1_%d1" % a, grouped=staging[a])
        first_stage(1)

        both_q = [None] * PASSES2
        drop_q = [None] * PASSES2

        def pair_up(b):
            pair = pairs[b][:].rearrange("p (t s m) -> p s t m", t=PACK, s=2)
            for t in range(PACK):
                nc.vector.tensor_copy(pair[:, 0, t, :], h[b, t][:].indirect(pos1_t[:]))
                nc.vector.tensor_copy(pair[:, 1, t, :], h[b, t][:].indirect(pos2_t[:]))
            core = pair[:, 0].rearrange("p t (c i) -> p c t i", i=2)
            surf = pair[:, 1].rearrange("p t (c i) -> p c t i", i=2)
            both = keep.tile([P, PACK * SECT], BF16, name="held", align_bytes=64)
            drop = keep.tile([P, PACK * SECT], BF16, name="late", align_bytes=64)
            nc.vector.tensor_tensor(both[:].rearrange("p (c i t) -> p c t i", i=2, t=PACK), core, surf, ALU.add)
            nc.vector.tensor_tensor(drop[:].rearrange("p (c i t) -> p c t i", i=2, t=PACK), core, surf, ALU.subtract)
            both_q[b] = quantize(both[:], "both%d" % b)
            drop_q[b] = quantize(drop[:], "drop%d" % b)

        def scale_by_gain(b, t):
            nc.scalar.activation(h[b, t][:], h[b, t][:], ACT.Copy, scale=gain_t[:, b, t : t + 1])

        wd_q = {}
        pair_up(0)
        for a in range(PASSES2):
            wd_q[a, 0] = prepare_weight(wd_raw[a, 0], "wd_%d0" % a)
        wd_grouped = [grp.tile([P, PACK * KP], BF16, name="grouped", align_bytes=64) for a in range(PASSES2)]
        for a in range(PASSES2):
            interleave_weight(wd_raw[a, 1], wd_grouped[a][:])
        for t in range(PACK):
            scale_by_gain(0, t)
        pair_up(1)
        for t in range(PACK):
            scale_by_gain(1, t)
        late_codes = keep.tile([P, PASSES2 * KP], U32, name="late", align_bytes=64)
        for a in range(PASSES2):
            wd_q[a, 1] = quantize(wd_grouped[a][:], "wd_%d1" % a, codes=late_codes[:, a * KP : (a + 1) * KP])

        order = [(b, t) for b in range(PASSES2) for t in range(PACK)]

        def second_stage(n):
            b, t = order[n]
            c0 = b * KP + t * P
            level = banks[n % 2]
            grad = banks[2 + n % 2]
            for a in range(PASSES2):
                nc.tensor.matmul_mx(
                    out=level[:],
                    lhsT=wsum_q[:, a, 2 * c0 : 2 * (c0 + P)].bitcast(FP4X4),
                    lhsT_scale=wsum_sc[:, a, c0 : c0 + P],
                    rhs=both_q[a][0][:].bitcast(FP8X4),
                    rhs_scale=both_q[a][1][:],
                    start=(a == 0),
                    stop=(a == PASSES2 - 1),
                )
            for a in range(PASSES2):
                codes, scales = wd_q[a, b]
                nc.tensor.matmul_mx(
                    out=grad[:],
                    lhsT=codes[:, t * P : (t + 1) * P].bitcast(FP8X4),
                    lhsT_scale=scales[:, t * P : (t + 1) * P],
                    rhs=drop_q[a][0][:].bitcast(FP8X4),
                    rhs_scale=drop_q[a][1][:],
                    start=(a == 0),
                    stop=(a == PASSES2 - 1),
                )
            y = windows[n % RING][:, SECT : 2 * SECT]
            nc.scalar.copy(y, level[:])
            nc.vector.tensor_tensor(y, grad[:], y, ALU.max)

        out_rows = out.rearrange("(b p t) j -> b t p j", p=P, t=PACK)
        second_stage(0)
        for n, (b, t) in enumerate(order):
            last = n == len(order) - 1
            if not last:
                second_stage(n + 1)
            window = windows[n % RING]
            square = keep.tile([P, SECT], F32, name="square")
            nc.scalar.activation(square[:], window[:, SECT : 2 * SECT], ACT.Square)
            nc.scalar.activation(window[:, :SECT], square[:], ACT.Ln, bias=1.0)
            result = rawp.tile([P, S], F32, name="raw")
            edges = (0, S // 2, 3 * S // 4, S) if last else (0, S)
            for c0, c1 in zip(edges, edges[1:]):
                cols = slice(c0, c1)
                entries = pos3_t[:, c0 // 16 : c1 // 16]
                nc.vector.tensor_tensor(result[:, cols], window[:].indirect(entries), h[b, t][:, cols], ALU.add)
                nc.sync.dma_start(out_rows[b, t][:, cols], result[:, cols])
